import numpy as np, ml_dtypes
CORES = [2,3,6,7,58,59,62,63,114,115,118,119]
N = 12
import mx_ref
NC = 384
WID = [354,366,354,314,244,152,292,366,288,128,384,342]
BF = ml_dtypes.bfloat16
def setup_inputs(rng):
    def f(*shape):
        return mx_ref.flush((rng.standard_normal(shape, dtype=np.float32) * np.exp2(rng.integers(-2, 3, shape[:-1] + (1,)))).astype(BF))
    return {"w": f(N, 128, 512), "x": f(N, 128, 4 * NC)}
def setup_inputs_blocks(rng):
    d = setup_inputs(rng)
    for k in ("w", "x"): d[k] = mx_ref.spread(d[k], rng, 4)
    return d
def setup_inputs_wide(rng):
    d = setup_inputs(rng)
    for k in ("w", "x"): d[k] = mx_ref.flush((d[k].astype(np.float32) * np.exp2(rng.integers(-8, 9, (N, 1, 1))).astype(np.float32)).astype(BF))
    return d
def reference(w, x):
    OFF = [sum(WID[:j]) for j in range(N + 1)]
    y = np.zeros((N, 128, OFF[N]), np.float32)
    for r in range(N):
        qw = mx_ref.quantize(w[r])
        for j in range(N):
            y[r][:, OFF[j]:OFF[j + 1]] = mx_ref.matmul(qw, mx_ref.quantize(x[j][:, :4 * WID[j]]))
    return {"y": y}

@@ -1,0 +1,158 @@
+from concourse.bass import DstId, RemoteDMATransfer
+from concourse.mybir import dt, ActivationFunctionType
+
+NT = 12
+YW = 3584
+BANK = 512
+NBANK = 8
+
+SCRATCH = {
+    "xb": ("sbuf", [128, 1536], "bfloat16"),
+    "wb": ("sbuf", [128, 512], "bfloat16"),
+    "wq": ("sbuf", [128, 128], "float8_e4m3fn_x4"),
+    "ws": ("sbuf", [128, 128], "uint8"),
+    "oq": ("sbuf", [128, 384], "float8_e4m3fn_x4"),
+    "oscl": ("sbuf", [128, 384], "uint8"),
+    "gq": ("sbuf", [128, YW], "float8_e4m3fn_x4"),
+    "gs": ("sbuf", [128, YW], "uint8"),
+    "ps": ("psum", [128, BANK * NBANK], "float32"),
+    "yb": ("sbuf", [128, YW], "float32"),
+}
+SEMAPHORES = (["ldx", "ldw", "qx", "qw", "sent", "st"] + ["a%d" % j for j in range(NT)]
+              + ["mm%d" % j for j in range(NT)] + ["cp%d" % j for j in range(NT)])
+CACHE = {}
+
+
+def nbits(m):
+    return bin(m).count("1")
+
+
+def make_plan(T, topo):
+    cores = [int(c) for c in T.cores]
+    wid = [int(v) for v in T.tables["WID"]]
+    n = len(cores)
+    chip = [topo.chip(c) for c in cores]
+    die = [topo.die(c) for c in cores]
+    chips = sorted(set(chip))
+    on = {ch: [r for r in range(n) if chip[r] == ch] for ch in chips}
+
+    groups = {}
+    for ch in chips:
+        gl = []
+        for d in sorted(set(die[r] for r in on[ch])):
+            takers = sorted([r for r in on[ch] if die[r] == d], key=lambda r: wid[r])
+            packs = [[j for j in on[s] if die[j] == d] for s in chips if s != ch]
+            packs.sort(key=lambda p: -sum(wid[j] for j in p))
+            gl += list(zip(takers, packs))
+        groups[ch] = gl
+
+    pos = {}
+    for ch in chips:
+        p, o = {}, 0
+        for j in [j for r, tl in groups[ch] for j in tl] + on[ch]:
+            p[j] = o
+            o += wid[j]
+        pos[ch] = p
+    off = [sum(wid[:j]) for j in range(n + 1)]
+    return {"cores": cores, "wid": wid, "chips": chips, "on": on, "groups": groups, "pos": pos, "off": off}
+
+
+def rank_program(g, core, T, topo):
+    rank = T.rank_of(core)
+    if rank is None:
+        return
+    if "plan" not in CACHE:
+        CACHE["plan"] = make_plan(T, topo)
+    P = CACHE["plan"]
+    cores, wid, on, pos, off = P["cores"], P["wid"], P["on"], P["pos"], P["off"]
+    ch = topo.chip(core)
+    sem = T.sem
+    n = wid[rank]
+    k = on[ch].index(rank)
+    peers = on[ch][k + 1:] + on[ch][:k]
+    mine = [tl for r, tl in P["groups"][ch] if r == rank][0]
+    sent = [0]
+
+    far = [c for c in cores if topo.chip(c) != ch][0]
+    m_all = topo.mask(core, cores[peers[0]])
+    m_off = topo.mask(core, far)
+    m_in = m_all & ~m_off
+
+    def send(src_q, src_s, s0, width, dsts, mask, name):
+        ids = []
+        for r, d0 in dsts:
+            rid, pid, se = topo.addr(cores[r])
+            ids.append(DstId(rid=rid, pnc=pid))
+        g.remote_dma_fused([RemoteDMATransfer(
+            dst_ids=ids, dma_engine_mask=mask, remote_sem=sem[name],
+            srcs=[src_q[:, s0:s0 + width].bitcast(dt.uint8)],
+            dsts=[T.gq[:, d0:d0 + width].bitcast(dt.uint8) for r, d0 in dsts])], local_sem=sem.sent)
+        g.remote_dma_fused([RemoteDMATransfer(
+            dst_ids=ids, dma_engine_mask=mask, remote_sem=sem[name],
+            srcs=[src_s[:, s0:s0 + width]],
+            dsts=[T.gs[:, d0:d0 + width] for r, d0 in dsts])], local_sem=sem.sent)
+        sent[0] += 2 * nbits(mask)
+
+    ready = {}
+    for r, tl in P["groups"][ch]:
+        for j in tl:
+            ready[j] = ("a%d" % j, 2 * nbits(m_off)) if r == rank else ("a%d" % tl[0], 2 * nbits(m_all))
+    for j in peers:
+        ready[j] = ("a%d" % j, 2 * nbits(m_in))
+
+    g.sync.dma_start(T.xb[:, 0:4 * n], T.x[:, 0:4 * n]).then_inc(sem.ldx, 16)
+    g.sync.dma_start(T.wb[:], T.w[:]).then_inc(sem.ldw, 16)
+    g.vector.wait_ge(sem.ldx, 16)
+    g.vector.quantize_mx(T.oq[:, 0:n], T.oscl[:, 0:n], T.xb[:, 0:4 * n]).then_inc(sem.qx, 1)
+    g.vector.wait_ge(sem.ldw, 16)
+    g.vector.quantize_mx(T.wq[:], T.ws[:], T.wb[:]).then_inc(sem.qw, 1)
+
+    away = []
+    for c2 in P["chips"]:
+        if c2 != ch:
+            away.append(([r for r, tl in P["groups"][c2] if rank in tl][0], pos[c2][rank]))
+    g.wait_ge(sem.qx, 1)
+    send(T.oq, T.oscl, 0, n, away, m_off, "a%d" % rank)
+    send(T.oq, T.oscl, 0, n, [(r, pos[ch][rank]) for r in peers], m_in, "a%d" % rank)
+    for j in mine:
+        g.wait_ge(sem[ready[j][0]], ready[j][1])
+    a = pos[ch][mine[0]]
+    send(T.gq, T.gs, a, sum(wid[j] for j in mine), [(r, a) for r in peers], m_all, "a%d" % mine[0])
+    g.wait_ge(sem.sent, sent[0])
+
+    rest = [tl for r, tl in P["groups"][ch] if r != rank]
+    rest.sort(key=lambda tl: 2.0 * max(wid[j] for j in tl) + 1.5 * sum(wid[j] for j in tl))
+    batches = [sorted(on[ch]), mine] + rest
+    seq = [rank] + sorted(peers, key=lambda j: wid[j]) + [j for tl in batches[1:] for j in sorted(tl, key=lambda j: wid[j])]
+
+    te = g.tensor
+    te.wait_ge(sem.qw, 1)
+    te.wait_ge(sem.qx, 1)
+    for i, j in enumerate(seq):
+        b = (i % NBANK) * BANK
+        if j != rank:
+            te.wait_ge(sem[ready[j][0]], ready[j][1])
+        if i >= NBANK:
+            te.wait_ge(sem["cp%d" % seq[i - NBANK]], 1)
+        if j == rank:
+            q, s = T.oq[:, 0:n], T.oscl[:, 0:n]
+        else:
+            q, s = T.gq[:, pos[ch][j]:pos[ch][j] + wid[j]], T.gs[:, pos[ch][j]:pos[ch][j] + wid[j]]
+        te.matmul_mx(T.ps[:, b:b + wid[j]], T.wq[:], T.ws[:], q, s, True, True).then_inc(sem["mm%d" % j], 1)
+
+    for i, j in enumerate(seq):
+        b = (i % NBANK) * BANK
+        dst, src = T.yb[:, off[j]:off[j + 1]], T.ps[:, b:b + wid[j]]
+        if i % 2 == 0:
+            g.vector.wait_ge(sem["mm%d" % j], 1)
+            g.vector.tensor_copy(dst, src).then_inc(sem["cp%d" % j], 1)
+        else:
+            g.scalar.wait_ge(sem["mm%d" % j], 1)
+            g.scalar.activation(dst, src, ActivationFunctionType.Copy).then_inc(sem["cp%d" % j], 1)
+
+    for tl in batches:
+        for j in tl:
+            g.sync.wait_ge(sem["cp%d" % j], 1)
+        lo, hi = off[min(tl)], off[max(tl) + 1]
+        g.sync.dma_start(T.y[:, lo:hi], T.yb[:, lo:hi]).then_inc(sem.st, 16)
+    g.sync.wait_ge(sem.st, 16 * len(batches))

@@ -3,6 +3,7 @@ from concourse.mybir import dt, ActivationFunctionType
 
 NT = 12
 YW = 3584
+NSIM = 128
 BANK = 512
 NBANK = 8
 
@@ -18,7 +19,7 @@ SCRATCH = {
     "ps": ("psum", [128, BANK * NBANK], "float32"),
     "yb": ("sbuf", [128, YW], "float32"),
 }
-SEMAPHORES = (["ldx", "ldw", "qx", "qw", "sent", "st"] + ["a%d" % j for j in range(NT)]
+SEMAPHORES = (["ldx", "ldw", "qx", "qw", "sent", "st"] + ["a%d" % j for j in range(NT)] + ["b%d" % j for j in range(NT)]
               + ["mm%d" % j for j in range(NT)] + ["cp%d" % j for j in range(NT)])
 CACHE = {}
 
@@ -35,95 +36,103 @@ def make_plan(T, topo):
     die = [topo.die(c) for c in cores]
     chips = sorted(set(chip))
     on = {ch: [r for r in range(n) if chip[r] == ch] for ch in chips}
+    ring = {ch: chips[i + 1:] + chips[:i] for i, ch in enumerate(chips)}
 
-    groups = {}
+    lands = {}
     for ch in chips:
-        gl = []
+        lands[ch] = {}
         for d in sorted(set(die[r] for r in on[ch])):
-            takers = sorted([r for r in on[ch] if die[r] == d], key=lambda r: wid[r])
-            packs = [[j for j in on[s] if die[j] == d] for s in chips if s != ch]
-            packs.sort(key=lambda p: -sum(wid[j] for j in p))
-            gl += list(zip(takers, packs))
-        groups[ch] = gl
-
-    pos = {}
-    for ch in chips:
-        p, o = {}, 0
-        for j in [j for r, tl in groups[ch] for j in tl] + on[ch]:
-            p[j] = o
-            o += wid[j]
-        pos[ch] = p
+            takers = sorted([cores[r] for r in on[ch] if die[r] == d], key=lambda c: wid[cores.index(c)])
+            takers += [c for c in range(NSIM) if topo.chip(c) == ch and topo.die(c) == d and c not in cores]
+            tiles = sorted([j for j in range(n) if chip[j] != ch and die[j] == d], key=lambda j: -wid[j])
+            for c, j in zip(takers, tiles):
+                lands[ch][j] = c
     off = [sum(wid[:j]) for j in range(n + 1)]
-    return {"cores": cores, "wid": wid, "chips": chips, "on": on, "groups": groups, "pos": pos, "off": off}
+    return {"cores": cores, "wid": wid, "chips": chips, "chip": chip, "die": die, "on": on, "ring": ring,
+            "lands": lands, "off": off}
 
 
 def rank_program(g, core, T, topo):
-    rank = T.rank_of(core)
-    if rank is None:
-        return
     if "plan" not in CACHE:
         CACHE["plan"] = make_plan(T, topo)
     P = CACHE["plan"]
-    cores, wid, on, pos, off = P["cores"], P["wid"], P["on"], P["pos"], P["off"]
     ch = topo.chip(core)
+    if ch not in P["chips"]:
+        return
+    cores, wid, on, off, lands = P["cores"], P["wid"], P["on"], P["off"], P["lands"]
+    rank = T.rank_of(core)
+    mine = [j for j in lands[ch] if lands[ch][j] == core]
     sem = T.sem
-    n = wid[rank]
-    k = on[ch].index(rank)
-    peers = on[ch][k + 1:] + on[ch][:k]
-    mine = [tl for r, tl in P["groups"][ch] if r == rank][0]
     sent = [0]
-
+    if rank is None:
+        peers = list(on[ch])
+    else:
+        k = on[ch].index(rank)
+        peers = on[ch][k + 1:] + on[ch][:k]
     far = [c for c in cores if topo.chip(c) != ch][0]
     m_all = topo.mask(core, cores[peers[0]])
-    m_off = topo.mask(core, far)
-    m_in = m_all & ~m_off
+    n_off = nbits(topo.mask(far, core))
 
-    def send(src_q, src_s, s0, width, dsts, mask, name):
+    def send(kind, src, s0, j, dsts, mask, name):
         ids = []
-        for r, d0 in dsts:
-            rid, pid, se = topo.addr(cores[r])
+        for c in dsts:
+            rid, pid, se = topo.addr(c)
             ids.append(DstId(rid=rid, pnc=pid))
-        g.remote_dma_fused([RemoteDMATransfer(
-            dst_ids=ids, dma_engine_mask=mask, remote_sem=sem[name],
-            srcs=[src_q[:, s0:s0 + width].bitcast(dt.uint8)],
-            dsts=[T.gq[:, d0:d0 + width].bitcast(dt.uint8) for r, d0 in dsts])], local_sem=sem.sent)
-        g.remote_dma_fused([RemoteDMATransfer(
-            dst_ids=ids, dma_engine_mask=mask, remote_sem=sem[name],
-            srcs=[src_s[:, s0:s0 + width]],
-            dsts=[T.gs[:, d0:d0 + width] for r, d0 in dsts])], local_sem=sem.sent)
-        sent[0] += 2 * nbits(mask)
+        if kind == "q":
+            tr = RemoteDMATransfer(dst_ids=ids, dma_engine_mask=mask, remote_sem=sem[name],
+                                   srcs=[src[:, s0:s0 + wid[j]].bitcast(dt.uint8)],
+                                   dsts=[T.gq[:, off[j]:off[j + 1]].bitcast(dt.uint8) for c in dsts])
+        else:
+            tr = RemoteDMATransfer(dst_ids=ids, dma_engine_mask=mask, remote_sem=sem[name],
+                                   srcs=[src[:, s0:s0 + wid[j]]], dsts=[T.gs[:, off[j]:off[j + 1]] for c in dsts])
+        g.remote_dma_fused([tr], local_sem=sem.sent)
+        sent[0] += nbits(mask)
+
+    if rank is not None:
+        n = wid[rank]
+        m_off = topo.mask(core, far)
+        m_in = m_all & ~m_off
+        g.sync.dma_start(T.xb[:, 0:4 * n], T.x[:, 0:4 * n]).then_inc(sem.ldx, 16)
+        g.sync.dma_start(T.wb[:], T.w[:]).then_inc(sem.ldw, 16)
+        g.vector.wait_ge(sem.ldx, 16)
+        g.vector.quantize_mx(T.oq[:, 0:n], T.oscl[:, 0:n], T.xb[:, 0:4 * n]).then_inc(sem.qx, 1)
+        g.vector.wait_ge(sem.ldw, 16)
+        g.vector.quantize_mx(T.wq[:], T.ws[:], T.wb[:]).then_inc(sem.qw, 1)
+        away = [lands[c2][rank] for c2 in P["ring"][ch]]
+        home = [cores[r] for r in peers]
+        g.wait_ge(sem.qx, 1)
+        send("q", T.oq, 0, rank, away, m_off, "a%d" % rank)
+        send("s", T.oscl, 0, rank, away, m_off, "b%d" % rank)
+        send("q", T.oq, 0, rank, home, m_in, "a%d" % rank)
+        send("s", T.oscl, 0, rank, home, m_in, "a%d" % rank)
+
+    for j in mine:
+        g.wait_ge(sem["a%d" % j], n_off)
+        send("q", T.gq, off[j], j, [cores[r] for r in peers], m_all, "a%d" % j)
+        g.wait_ge(sem["b%d" % j], n_off)
+        send("s", T.gs, off[j], j, [cores[r] for r in peers], m_all, "a%d" % j)
+    g.wait_ge(sem.sent, sent[0])
+    if rank is None:
+        return
 
     ready = {}
-    for r, tl in P["groups"][ch]:
-        for j in tl:
-            ready[j] = ("a%d" % j, 2 * nbits(m_off)) if r == rank else ("a%d" % tl[0], 2 * nbits(m_all))
+    for j in lands[ch]:
+        ready[j] = [("a%d" % j, n_off), ("b%d" % j, n_off)] if j in mine else [("a%d" % j, 2 * nbits(m_all))]
     for j in peers:
-        ready[j] = ("a%d" % j, 2 * nbits(m_in))
+        ready[j] = [("a%d" % j, 2 * nbits(m_in))]
 
-    g.sync.dma_start(T.xb[:, 0:4 * n], T.x[:, 0:4 * n]).then_inc(sem.ldx, 16)
-    g.sync.dma_start(T.wb[:], T.w[:]).then_inc(sem.ldw, 16)
-    g.vector.wait_ge(sem.ldx, 16)
-    g.vector.quantize_mx(T.oq[:, 0:n], T.oscl[:, 0:n], T.xb[:, 0:4 * n]).then_inc(sem.qx, 1)
-    g.vector.wait_ge(sem.ldw, 16)
-    g.vector.quantize_mx(T.wq[:], T.ws[:], T.wb[:]).then_inc(sem.qw, 1)
-
-    away = []
-    for c2 in P["chips"]:
-        if c2 != ch:
-            away.append(([r for r, tl in P["groups"][c2] if rank in tl][0], pos[c2][rank]))
-    g.wait_ge(sem.qx, 1)
-    send(T.oq, T.oscl, 0, n, away, m_off, "a%d" % rank)
-    send(T.oq, T.oscl, 0, n, [(r, pos[ch][rank]) for r in peers], m_in, "a%d" % rank)
-    for j in mine:
-        g.wait_ge(sem[ready[j][0]], ready[j][1])
-    a = pos[ch][mine[0]]
-    send(T.gq, T.gs, a, sum(wid[j] for j in mine), [(r, a) for r in peers], m_all, "a%d" % mine[0])
-    g.wait_ge(sem.sent, sent[0])
-
-    rest = [tl for r, tl in P["groups"][ch] if r != rank]
-    rest.sort(key=lambda tl: 2.0 * max(wid[j] for j in tl) + 1.5 * sum(wid[j] for j in tl))
-    batches = [sorted(on[ch]), mine] + rest
-    seq = [rank] + sorted(peers, key=lambda j: wid[j]) + [j for tl in batches[1:] for j in sorted(tl, key=lambda j: wid[j])]
+    def eta(j):
+        if j in mine:
+            return 0
+        place = P["ring"][P["chip"][j]].index(ch)
+        return (2.0 * place + (3.5 if lands[ch][j] in cores else 3.0)) * wid[j]
+    batches = []
+    for c2 in P["ring"][ch]:
+        for d in sorted(set(P["die"][j] for j in on[c2])):
+            batches.append([j for j in on[c2] if P["die"][j] == d])
+    batches.sort(key=lambda tl: max(eta(j) for j in tl))
+    batches = [sorted(on[ch])] + batches
+    seq = [rank] + sorted(peers, key=lambda j: wid[j]) + sorted(lands[ch], key=eta)
 
     te = g.tensor
     te.wait_ge(sem.qw, 1)
@@ -131,13 +140,14 @@ def rank_program(g, core, T, topo):
     for i, j in enumerate(seq):
         b = (i % NBANK) * BANK
         if j != rank:
-            te.wait_ge(sem[ready[j][0]], ready[j][1])
+            for name, v in ready[j]:
+                te.wait_ge(sem[name], v)
         if i >= NBANK:
             te.wait_ge(sem["cp%d" % seq[i - NBANK]], 1)
         if j == rank:
             q, s = T.oq[:, 0:n], T.oscl[:, 0:n]
         else:
-            q, s = T.gq[:, pos[ch][j]:pos[ch][j] + wid[j]], T.gs[:, pos[ch][j]:pos[ch][j] + wid[j]]
+            q, s = T.gq[:, off[j]:off[j + 1]], T.gs[:, off[j]:off[j + 1]]
         te.matmul_mx(T.ps[:, b:b + wid[j]], T.wq[:], T.ws[:], q, s, True, True).then_inc(sem["mm%d" % j], 1)
 
     for i, j in enumerate(seq):

from concourse.bass import DstId, RemoteDMATransfer
from concourse.mybir import dt, ActivationFunctionType

NT = 12
YW = 3584
NSIM = 128
BANK = 512
NBANK = 8

SCRATCH = {
    "xb": ("sbuf", [128, 1536], "bfloat16"),
    "wb": ("sbuf", [128, 512], "bfloat16"),
    "wq": ("sbuf", [128, 128], "float8_e4m3fn_x4"),
    "ws": ("sbuf", [128, 128], "uint8"),
    "oq": ("sbuf", [128, 384], "float8_e4m3fn_x4"),
    "oscl": ("sbuf", [128, 384], "uint8"),
    "gq": ("sbuf", [128, YW], "float8_e4m3fn_x4"),
    "gs": ("sbuf", [128, YW], "uint8"),
    "ps": ("psum", [128, BANK * NBANK], "float32"),
    "yb": ("sbuf", [128, YW], "float32"),
}
SEMAPHORES = (["ldx", "ldw", "qx", "qw", "sent", "st"] + ["a%d" % j for j in range(NT)] + ["b%d" % j for j in range(NT)]
              + ["mm%d" % j for j in range(NT)] + ["cp%d" % j for j in range(NT)])
CACHE = {}


def nbits(m):
    return bin(m).count("1")


def make_plan(T, topo):
    cores = [int(c) for c in T.cores]
    wid = [int(v) for v in T.tables["WID"]]
    n = len(cores)
    chip = [topo.chip(c) for c in cores]
    die = [topo.die(c) for c in cores]
    chips = sorted(set(chip))
    on = {ch: [r for r in range(n) if chip[r] == ch] for ch in chips}
    ring = {ch: chips[i + 1:] + chips[:i] for i, ch in enumerate(chips)}

    lands = {}
    for ch in chips:
        lands[ch] = {}
        for d in sorted(set(die[r] for r in on[ch])):
            takers = sorted([cores[r] for r in on[ch] if die[r] == d], key=lambda c: wid[cores.index(c)])
            takers += [c for c in range(NSIM) if topo.chip(c) == ch and topo.die(c) == d and c not in cores]
            tiles = sorted([j for j in range(n) if chip[j] != ch and die[j] == d], key=lambda j: -wid[j])
            for c, j in zip(takers, tiles):
                lands[ch][j] = c
    off = [sum(wid[:j]) for j in range(n + 1)]
    return {"cores": cores, "wid": wid, "chips": chips, "chip": chip, "die": die, "on": on, "ring": ring,
            "lands": lands, "off": off}


def rank_program(g, core, T, topo):
    if "plan" not in CACHE:
        CACHE["plan"] = make_plan(T, topo)
    P = CACHE["plan"]
    ch = topo.chip(core)
    if ch not in P["chips"]:
        return
    cores, wid, on, off, lands = P["cores"], P["wid"], P["on"], P["off"], P["lands"]
    rank = T.rank_of(core)
    mine = [j for j in lands[ch] if lands[ch][j] == core]
    sem = T.sem
    sent = [0]
    if rank is None:
        peers = list(on[ch])
    else:
        k = on[ch].index(rank)
        peers = on[ch][k + 1:] + on[ch][:k]
    far = [c for c in cores if topo.chip(c) != ch][0]
    m_all = topo.mask(core, cores[peers[0]])
    n_off = nbits(topo.mask(far, core))

    def send(kind, src, s0, j, dsts, mask, name):
        ids = []
        for c in dsts:
            rid, pid, se = topo.addr(c)
            ids.append(DstId(rid=rid, pnc=pid))
        if kind == "q":
            tr = RemoteDMATransfer(dst_ids=ids, dma_engine_mask=mask, remote_sem=sem[name],
                                   srcs=[src[:, s0:s0 + wid[j]].bitcast(dt.uint8)],
                                   dsts=[T.gq[:, off[j]:off[j + 1]].bitcast(dt.uint8) for c in dsts])
        else:
            tr = RemoteDMATransfer(dst_ids=ids, dma_engine_mask=mask, remote_sem=sem[name],
                                   srcs=[src[:, s0:s0 + wid[j]]], dsts=[T.gs[:, off[j]:off[j + 1]] for c in dsts])
        g.remote_dma_fused([tr], local_sem=sem.sent)
        sent[0] += nbits(mask)

    if rank is not None:
        n = wid[rank]
        m_off = topo.mask(core, far)
        m_in = m_all & ~m_off
        g.sync.dma_start(T.xb[:, 0:4 * n], T.x[:, 0:4 * n]).then_inc(sem.ldx, 16)
        g.sync.dma_start(T.wb[:], T.w[:]).then_inc(sem.ldw, 16)
        g.vector.wait_ge(sem.ldx, 16)
        g.vector.quantize_mx(T.oq[:, 0:n], T.oscl[:, 0:n], T.xb[:, 0:4 * n]).then_inc(sem.qx, 1)
        g.vector.wait_ge(sem.ldw, 16)
        g.vector.quantize_mx(T.wq[:], T.ws[:], T.wb[:]).then_inc(sem.qw, 1)
        away = [lands[c2][rank] for c2 in P["ring"][ch]]
        home = [cores[r] for r in peers]
        g.wait_ge(sem.qx, 1)
        send("q", T.oq, 0, rank, away, m_off, "a%d" % rank)
        send("s", T.oscl, 0, rank, away, m_off, "b%d" % rank)
        send("q", T.oq, 0, rank, home, m_in, "a%d" % rank)
        send("s", T.oscl, 0, rank, home, m_in, "a%d" % rank)

    for j in mine:
        g.wait_ge(sem["a%d" % j], n_off)
        send("q", T.gq, off[j], j, [cores[r] for r in peers], m_all, "a%d" % j)
        g.wait_ge(sem["b%d" % j], n_off)
        send("s", T.gs, off[j], j, [cores[r] for r in peers], m_all, "a%d" % j)
    g.wait_ge(sem.sent, sent[0])
    if rank is None:
        return

    ready = {}
    for j in lands[ch]:
        ready[j] = [("a%d" % j, n_off), ("b%d" % j, n_off)] if j in mine else [("a%d" % j, 2 * nbits(m_all))]
    for j in peers:
        ready[j] = [("a%d" % j, 2 * nbits(m_in))]

    def eta(j):
        if j in mine:
            return 0
        place = P["ring"][P["chip"][j]].index(ch)
        return (2.0 * place + (3.5 if lands[ch][j] in cores else 3.0)) * wid[j]
    batches = []
    for c2 in P["ring"][ch]:
        for d in sorted(set(P["die"][j] for j in on[c2])):
            batches.append([j for j in on[c2] if P["die"][j] == d])
    batches.sort(key=lambda tl: max(eta(j) for j in tl))
    batches = [sorted(on[ch])] + batches
    seq = [rank] + sorted(peers, key=lambda j: wid[j]) + sorted(lands[ch], key=eta)

    te = g.tensor
    te.wait_ge(sem.qw, 1)
    te.wait_ge(sem.qx, 1)
    for i, j in enumerate(seq):
        b = (i % NBANK) * BANK
        if j != rank:
            for name, v in ready[j]:
                te.wait_ge(sem[name], v)
        if i >= NBANK:
            te.wait_ge(sem["cp%d" % seq[i - NBANK]], 1)
        if j == rank:
            q, s = T.oq[:, 0:n], T.oscl[:, 0:n]
        else:
            q, s = T.gq[:, off[j]:off[j + 1]], T.gs[:, off[j]:off[j + 1]]
        te.matmul_mx(T.ps[:, b:b + wid[j]], T.wq[:], T.ws[:], q, s, True, True).then_inc(sem["mm%d" % j], 1)

    for i, j in enumerate(seq):
        b = (i % NBANK) * BANK
        dst, src = T.yb[:, off[j]:off[j + 1]], T.ps[:, b:b + wid[j]]
        if i % 2 == 0:
            g.vector.wait_ge(sem["mm%d" % j], 1)
            g.vector.tensor_copy(dst, src).then_inc(sem["cp%d" % j], 1)
        else:
            g.scalar.wait_ge(sem["mm%d" % j], 1)
            g.scalar.activation(dst, src, ActivationFunctionType.Copy).then_inc(sem["cp%d" % j], 1)

    for tl in batches:
        for j in tl:
            g.sync.wait_ge(sem["cp%d" % j], 1)
        lo, hi = off[min(tl)], off[max(tl) + 1]
        g.sync.dma_start(T.y[:, lo:hi], T.yb[:, lo:hi]).then_inc(sem.st, 16)
    g.sync.wait_ge(sem.st, 16 * len(batches))
